import numpy as np
import ml_dtypes


def mxq(x, axis, fmt="e4m3"):
    dtype, down = {"e4m3": (ml_dtypes.float8_e4m3fn, 7), "e5m2": (ml_dtypes.float8_e5m2, 14)}[fmt]
    v = np.moveaxis(np.asarray(x, np.float32).astype(ml_dtypes.bfloat16).astype(np.float64), axis, -1)
    blocks = v.reshape(v.shape[:-1] + (-1, 32))
    amax = np.abs(blocks).max(-1, keepdims=True)
    byte = np.maximum(np.where(amax > 0, np.frexp(amax)[1] - 1 + 127, 0) - down, 1)
    scale = np.exp2(byte - 127.0)
    codes = (blocks / scale).astype(np.float32).astype(dtype).astype(np.float64)
    return np.moveaxis((codes * scale).reshape(v.shape), -1, axis)


WIDE = False


def mx_kscale(k):
    if not WIDE:
        return np.ones(k)
    levels = np.array([10, -10, 5, -5, 0])
    if k % 512:
        return np.exp2(np.random.permutation(np.resize(levels, k // 32))).repeat(32)
    a = np.empty((k // 512, 16))
    for p in range(k // 512):
        a[p, :8] = np.random.permutation(np.resize(levels, 8))
        for g in range(8):
            far = levels[np.abs(levels - a[p, g]) >= 10]
            a[p, g + 8] = far[np.random.randint(len(far))]
    return np.exp2(a.ravel()).repeat(32)


BF16 = ml_dtypes.bfloat16


def bf(x):
    return np.asarray(x, np.float32).astype(BF16)


def f64(x):
    return np.asarray(x).astype(np.float64)


E2M1 = np.array([0.0, 0.5, 1.0, 1.5, 2.0, 3.0, 4.0, 6.0, -0.0, -0.5, -1.0, -1.5, -2.0, -3.0, -4.0, -6.0])


def pack_weight(w, fmt):
    k, n = w.shape
    w = f64(bf(w)).reshape(k // 32, 32, n)
    amax = np.abs(w).max(1)
    if fmt == "e4m3":
        byte = np.frexp(amax)[1] - 1 + 127 - 7
    else:
        mant, ex = np.frexp(amax / 6.0)
        byte = np.where(mant > 0.5, ex, ex - 1) + 127
    byte = np.clip(np.where(amax > 0, byte, 1), 1, 254)
    scaled = (w * np.exp2(127.0 - byte)[:, None, :]).reshape(k, n).astype(np.float32)
    by_word = np.ascontiguousarray(scaled.reshape(k // 512, 128, 4, n).transpose(0, 1, 3, 2))
    if fmt == "e4m3":
        words = by_word.astype(ml_dtypes.float8_e4m3fn).view(np.uint8)
    else:
        c = by_word.astype(ml_dtypes.float4_e2m1fn).view(np.uint8) & 0xF
        words = c[..., 0::2] | (c[..., 1::2] << 4)
    return np.ascontiguousarray(words), np.ascontiguousarray(byte.astype(np.uint8).reshape(k // 512, 16, n))


def unpack_weight(words, scales, fmt):
    g, p, n, _ = words.shape
    if fmt == "e4m3":
        vals = np.ascontiguousarray(words).view(ml_dtypes.float8_e4m3fn).astype(np.float64)
    else:
        nib = np.empty((g, p, n, 4), np.uint8)
        nib[..., 0::2] = words & 0xF
        nib[..., 1::2] = words >> 4
        vals = E2M1[nib]
    vals = vals * np.repeat(np.exp2(scales.astype(np.float64) - 127.0), 8, axis=1)[..., None]
    return vals.transpose(0, 1, 3, 2).reshape(g * 512, n)
def pack4(w):
    words, scales = pack_weight(w, "e2m1")
    return words.reshape(words.shape[0], 128, -1), scales


def unpack4(words, scales):
    return unpack_weight(words.reshape(words.shape[0], 128, -1, 2), scales, "e2m1")


def planes(Y):
    n, m = Y.shape
    b = f64(bf(Y)).reshape(n // 32, 32, m)
    amax = np.abs(b).max(1)
    byte = np.clip(np.where(amax > 0, np.frexp(amax)[1] - 1 + 127 - 7, 1), 1, 254)
    codes = (b * np.exp2(127.0 - byte)[:, None, :]).reshape(n, m).astype(np.float32).astype(ml_dtypes.float8_e4m3fn).view(np.uint8)
    words = codes.reshape(n // 512, 128, 4, m).transpose(0, 1, 3, 2)
    return np.ascontiguousarray(words), np.ascontiguousarray(byte.astype(np.uint8).reshape(n // 512, 16, m))


NE, NT, K, D = 1024, 2048, 1024, 512

def setup_inputs():
    s, t = mx_kscale(K), mx_kscale(D)
    psi = 0.2 * np.exp(0.3 * np.random.randn(D))
    half = 0.5 * psi ** 2 / ((2 * psi + 1) * (psi + 1))
    w = np.sqrt(psi / (2 * psi + 1) / half)
    W = np.random.randn(K, D) * np.sqrt((psi + 1) * half)[None, :] / np.sqrt(K)
    E = np.random.randn(NE, K)
    X = np.random.randn(K, NT)
    const = 0.5 * np.sum(np.log((psi + 1) ** 2 / (2 * psi + 1)))
    offset = const + np.random.randn(NE)
    gain = 0.2 * np.exp(0.8 * np.random.randn(NE))
    test_words, test_scales = pack_weight(X / s[:, None], "e4m3")
    proj_words, proj_scales = pack4(W * s[:, None])
    return {"enrol": bf(E / s[None, :]), "test_words": test_words, "test_scales": test_scales,
            "proj_words": proj_words, "proj_scales": proj_scales,
            "w_enrol": bf(w * t), "w_test": bf(w / t), "offset": bf(offset), "gain": bf(gain)}

def reference(enrol, test_words, test_scales, proj_words, proj_scales, w_enrol, w_test, offset, gain):
    W = unpack4(proj_words, proj_scales)
    X = unpack_weight(test_words, test_scales, "e4m3")
    U = mxq(f64(enrol), 1, "e4m3") @ W
    V = X.T @ W
    self_e = (U * U).sum(axis=1)
    self_x = (V * V).sum(axis=1)
    A = U * f64(w_enrol)
    B = V * f64(w_test)
    C = mxq(B, 1, "e4m3") @ mxq(A, 1, "e4m3").T
    y = (C - self_x[:, None] - self_e[None, :] + f64(offset)) * f64(gain)
    words, scales = planes(y.T)
    return y, words, scales

from contextlib import ExitStack

import concourse.mybir as mybir
from concourse.masks import make_identity

NE, NT, K, D = 1024, 2048, 1024, 512
FLOPS = 2 * (NE * K * D + NT * K * D + NT * D * NE)

F32 = mybir.dt.float32
BF16 = mybir.dt.bfloat16
I32 = mybir.dt.int32
U32 = mybir.dt.uint32
U8 = mybir.dt.uint8
FP8X4 = mybir.dt.float8_e4m3fn_x4
FP4X4 = mybir.dt.float4_e2m1fn_x4
ALU = mybir.AluOpType
ACT = mybir.ActivationFunctionType

P = 128
PACK = 4
SPAN = P * PACK
PASSES = K // SPAN
GROUPS = NE // SPAN
CHUNKS = NT // SPAN
BANKS = 8
PARTS = 4
SET_ORDER = [0,2,3,1,4,5]
BLOCKS = [[0,0],[0,1],[1,0],[1,1],[0,2],[1,2],[0,3],[1,3]]
ORDER = """
E0 w0 E1 E0.cS W0 E1.cS E0.q E3 w1 W0.cS W1 E1.q E3.cS P00 W1.cS P01 E3.q P00.s P21 P01.m P20 P21.m P03 P01.s
P20.m E2 P21.s P00.m P20.s E4 P03.m A00 E2.cS E4.cV E6 A00.cS P23 E2.q P03.s E4.q A00.q P22 P23.m E6.cS P02
P22.m A20 P23.s P02.m E5 P22.s A20.cV A21 P02.s A01 E6.q E7 A20.q A21.cS A01.cV H0 X0 E5.cS A21.q P31 E7.cS
A01.q X0.cV P32 P31.s E7.q C00 E5.q P30 P32.s T02G P31.m P33 T01S P30.m T00G P11 P33.s P32.m C01 T03G P10
C00.y P30.s C03 P33.m P11.s C02 A30 C03.y P10.s A31 P11.m A30.cS X1 P10.m A31.cS P40 A30.q X1.cS C01.y P40.s
A31.q P41 C02.y T13G T11S P13 P40.m T12G T10S P41.m C11 C13 P13.s I02G P12 C11.y P41.s C12 C13.y I03G C10
P12.s A10 P13.m A40 C10.y H1 A10.cS Y03 P12.m Y02 T22G A40.cS Y00 Y03.cV Y02.cS A11 T20G C12.y Y00.cS Y03.d
Y02.d A10.q A11.cS Y13 A40.q Y00.d I00V Y11 T23S I10V Y12 Y10 A11.q Y13.cS Y11.cV P42 T21G Y10.cS Y13.d P43
I01V Y11.d P42.s T32V Y10.d P53 Q0 Y12.cS P50 P42.m T33G P43.s Q0.d P52 Y12.d P53.m I12G P50.s P51 P43.m P53.s
C20 I13G P52.m C23 P51.s C21 P50.m C22 T31G P52.s A51 C23.y X2 T30G I11S P51.m A51.cS C20.y A50 Q1 X2.cS A51.q
A50.cS Q1.d C22.y T51G Y01 T50S C32 C21.y T53G T52S C31 Y01.cV C30 I22S T42G C32.y C33 Y01.d Y21 I21S A50.q
Y22 C30.y I23G Y21.cS A41 C31.y Y20 Y22.cS I20G Y23 Y21.d C33.y A41.cS X3 Y22.d T40V Y23.cS T43V Y31 A41.q Y30
Y20.cS T41V Y32 Y23.d Q2 X3.cS C42 Y20.d Y30.cV I32G C43 Y32.cS Q2.d C41 C42.y C53 T61S Y30.d T62G C40 Y32.d
C43.y Y31.cS T72G C53.y T70S C40.y C52 Y31.d T71G T73S C51 C41.y C50 I31G I33S C52.y Y42 I43S I40G C50.y Y40
Y43 Y42.cV I42G Y40.cS Y41 C51.y C70 Y43.cS Y42.d C73 I41V Y40.d C71 I52S I51V C72 Y43.d Q4 Y52 Y41.cS C73.y
Y53 I53G Q4.d Y52.cS Y51 Y41.d C70.y Y50 I50G Y53.cS C71.y Y52.d Y33 Y51.cS C72.y C62 Y53.d Y50.cS C61 Q5
Y51.d C63 Y33.cS C60 T63V Y50.d Y70 T60V Q5.d I73S I30V Y33.d Y72 I71G Y70.cS Y71 C61.y Y73 Y72.cS C60.y I72G
Y70.d Y73.cS C63.y Y72.d I70G Y71.cS C62.y Y73.d Q3 Y71.d Y61 Q7 Y62 I60S Q3.d Y63 Y61.cV I61G Y60 Q7.d I63S
Z12 Z13 Y63.cV Z11 Z10 Y60.cS Y61.d Y62.cV Y63.d I62V Y62.d Q6 Y60.d Z00 Z01 Z02 Z03 Q6.d
"""


def tile_plda_trial_scores_k4_kernel(
    tc, enrol, test_words, test_scales, proj_words, proj_scales, w_enrol, w_test, offset, gain, out_0, out_1, out_2
):
    nc = tc.nc
    with ExitStack() as ctx:
        keep = ctx.enter_context(tc.tile_pool(name="keep", bufs=1))
        psum = ctx.enter_context(tc.psum_pool(name="psum", bufs=1))
        ctx.enter_context(tc.manual_schedule())

        def tiles(name, count, shape, dtype):
            return [keep.tile(shape, dtype, name="%s%d" % (name, n), align_bytes=64) for n in range(count)]

        banks = [psum.tile([P, SPAN], F32, name="bank%d" % n) for n in range(BANKS)]
        ident = keep.tile([P, P], F32, name="ident")
        w_words = keep.tile([P, PASSES, 2 * D], U8, name="w_words", align_bytes=64)
        w_scales = keep.tile([P, PASSES, D], U8, name="w_scales", align_bytes=64)
        x_words = tiles("x_words", CHUNKS, [P, PASSES, SPAN], U32)
        x_scales = keep.tile([P, PASSES, NT], U8, name="x_scales", align_bytes=64)
        e_raw = tiles("e_raw", GROUPS, [P, PACK, K], BF16)
        e_grouped = tiles("e_grouped", 3, [P, K], BF16)
        e_words = tiles("e_words", GROUPS * PACK, [P, PASSES * P], U32)
        e_scales = tiles("e_scales", GROUPS * PACK, [P, PASSES * P], U8)
        weight_raw = tiles("weight_raw", 2, [P, PACK], BF16)
        weight_cols = tiles("weight_cols", 2, [P, PACK], F32)
        weight_rows = tiles("weight_rows", 2, [P, D], F32)
        offset_cols = keep.tile([P, GROUPS, PACK], BF16, name="offset_cols")
        gain_cols = keep.tile([P, GROUPS, PACK], BF16, name="gain_cols")
        minus_gain = keep.tile([P, GROUPS, PACK], F32, name="minus_gain")
        shift = tiles("shift", GROUPS, [P, PACK], F32)
        self_cols = tiles("self_cols", GROUPS + CHUNKS, [P, PACK], F32)
        squares = tiles("squares", 2, [P, D], BF16)
        scaled = tiles("scaled", 6, [P, D], BF16)
        ab_grouped = tiles("ab_grouped", 3, [P, 2 * SPAN], BF16)
        ab_words = tiles("ab_words", GROUPS + CHUNKS, [P, SPAN], U32)
        ab_scales = tiles("ab_scales", GROUPS + CHUNKS, [P, SPAN], U8)
        self_x_rows = tiles("self_x_rows", CHUNKS, [P, SPAN], F32)
        terms = tiles("terms", 16, [P, SPAN], F32)
        scores = tiles("scores", 3, [P, PACK, SPAN], F32)
        score_rows = tiles("score_rows", 12, [P, SPAN], F32)
        y_grouped = tiles("y_grouped", 3, [P, SPAN, PACK], BF16)
        y_words = tiles("y_words", GROUPS * CHUNKS, [P, SPAN], U32)
        y_scales = tiles("y_scales", GROUPS, [P, NT], U8)
        scaled_shift = tiles("scaled_shift", GROUPS, [P, PACK], F32)

        engines = {"S": nc.scalar, "V": nc.vector, "G": nc.gpsimd}

        def copy(engine, out, in_):
            if engine == "S":
                nc.scalar.copy(out=out, in_=in_)
            elif engine == "V":
                nc.vector.tensor_copy(out=out, in_=in_)
            else:
                nc.gpsimd.tensor_scalar(out=out, in0=in_, scalar1=1.0, scalar2=0.0, op0=ALU.mult, op1=ALU.add)

        def quantize(words, scales, values):
            nc.vector.quantize_mx(out=words.bitcast(FP8X4), scales=scales, in_=values)

        def load_scales(plane, rows):
            for q in range(4):
                nc.sync.dma_start(
                    out=plane[32 * q : 32 * q + 4, :, :].bitcast(I32),
                    in_=rows[:, 4 * q : 4 * q + 4, :].rearrange("h r n -> r h n").bitcast(I32),
                )

        def load_enrol(g, t0, t1):
            rows = enrol[SPAN * g : SPAN * (g + 1), :].rearrange("(p t) k -> p t k", t=PACK)
            nc.sync.dma_start(out=e_raw[g][:, t0:t1, :], in_=rows[:, t0:t1, :])

        def load_test(c):
            src = test_words.rearrange("h p n t -> p h (n t)")[:, :, PACK * SPAN * c : PACK * SPAN * (c + 1)]
            nc.sync.dma_start(out=x_words[c][:].bitcast(I32), in_=src.bitcast(I32))

        held = {}

        def claim(key):
            held[key] = banks[len(held) % BANKS]
            return held[key]

        def transposes(key, sources):
            bank = claim(key)
            for n, source in enumerate(sources):
                nc.tensor.transpose(bank[:, P * n : P * (n + 1)], source, ident[:])

        def widen_weight(side, engine):
            nc.vector.tensor_copy(out=weight_cols[side][:], in_=weight_raw[side][:])

        def spread_weight(side, engine):
            transposes(("W", side), [weight_cols[side][:, t : t + 1].to_broadcast([P, P]) for t in range(PACK)])

        def copy_weight(side, engine):
            copy(engine, weight_rows[side][:].rearrange("i (u p e) -> i u p e", u=2, e=2),
                 held[("W", side)][:].rearrange("i (u e p) -> i u p e", u=2, e=2))

        def turn_enrol(n, engine):
            words = e_raw[n // PACK][:, n % PACK, :].bitcast(F32)
            transposes(("E", n), [words[:, 2 * P * h + u : 2 * P * (h + 1) : 2] for h in range(PASSES) for u in range(2)])

        def copy_enrol(n, engine):
            copy(engine, e_grouped[n % 3][:].bitcast(F32).rearrange("p (h r u) -> p h r u", h=PASSES, u=2),
                 held[("E", n)][:].rearrange("p (h u r) -> p h r u", h=PASSES, u=2))

        def quantize_enrol(n, engine):
            quantize(e_words[n][:], e_scales[n][:], e_grouped[n % 3][:])

        def project(s, a, engine):
            bank = claim(("P", s, a))
            for h in range(PASSES):
                if s < GROUPS:
                    words = e_words[PACK * s + a][:, P * h : P * (h + 1)]
                    scales = e_scales[PACK * s + a][:, P * h : P * (h + 1)]
                else:
                    c = s - GROUPS
                    words = x_words[c][:, h, P * a : P * (a + 1)]
                    scales = x_scales[:, h, SPAN * c + P * a : SPAN * c + P * (a + 1)]
                nc.tensor.matmul_mx(
                    out=bank[:], lhsT=words.bitcast(FP8X4), lhsT_scale=scales,
                    rhs=w_words[:, h, :].bitcast(FP4X4), rhs_scale=w_scales[:, h, :],
                    start=(h == 0), stop=(h == PASSES - 1),
                )

        def tile_number(s, a):
            return PACK * SET_ORDER.index(s) + a

        def sum_squares(s, a, engine):
            nc.scalar.activation(
                out=squares[a % 2][:], in_=held[("P", s, a)][:], func=ACT.Square, accum_out=self_cols[s][:, a : a + 1]
            )

        def weigh(s, a, engine):
            nc.vector.tensor_tensor(
                out=scaled[tile_number(s, a) % 6][:].rearrange("i (u p e) -> i u p e", u=2, e=2),
                in0=held[("P", s, a)][:].rearrange("i (p u e) -> i u p e", u=2, e=2),
                in1=weight_rows[0 if s < GROUPS else 1][:].rearrange("i (u p e) -> i u p e", u=2, e=2),
                op=ALU.mult,
            )

        def turn_scaled(s, half, engine):
            pair = [scaled[tile_number(s, 2 * half + b) % 6][:].bitcast(F32) for b in range(2)]
            transposes(("A", s, half), [words[:, P * u : P * (u + 1)] for words in pair for u in range(2)])

        def copy_scaled(s, half, engine):
            grouped = ab_grouped[tile_number(s, 2 * half) // 2 % 3]
            copy(engine, grouped[:].bitcast(F32).rearrange("p (b r u) -> p b r u", b=2, u=2),
                 held[("A", s, half)][:].rearrange("p (b u r) -> p b r u", b=2, u=2))

        def quantize_scaled(s, half, engine):
            cols = slice(2 * P * half, 2 * P * (half + 1))
            quantize(ab_words[s][:, cols], ab_scales[s][:, cols], ab_grouped[tile_number(s, 2 * half) // 2 % 3][:])

        def spread_self_x(c, engine):
            transposes(("X", c), [self_cols[GROUPS + c][:, a : a + 1].to_broadcast([P, P]) for a in range(PACK)])

        def copy_self_x(c, engine):
            copy(engine, self_x_rows[c][:], held[("X", c)][:])

        def make_shift(g, engine):
            if g == 0:
                nc.gpsimd.tensor_scalar(out=minus_gain[:], in0=gain_cols[:], scalar1=-1.0, scalar2=0.0, op0=ALU.mult, op1=ALU.add)
            nc.gpsimd.tensor_tensor(out=shift[g][:], in0=self_cols[g][:], in1=offset_cols[:, g, :], op=ALU.subtract)
            nc.gpsimd.tensor_tensor(out=scaled_shift[g][:], in0=shift[g][:], in1=minus_gain[:, g, :], op=ALU.mult)

        def make_term(b, t, engine):
            g, c = BLOCKS[b]
            term = terms[(PACK * b + t) % 16]
            if engine == "S":
                nc.scalar.activation(out=term[:], in_=self_x_rows[c][:], func=ACT.Identity,
                                     scale=minus_gain[:, g, t : t + 1], bias=scaled_shift[g][:, t : t + 1])
            else:
                engines[engine].tensor_scalar(out=term[:], in0=self_x_rows[c][:], scalar1=minus_gain[:, g, t : t + 1],
                                              scalar2=scaled_shift[g][:, t : t + 1], op0=ALU.mult, op1=ALU.add)

        def cross(b, t, engine):
            g, c = BLOCKS[b]
            cols = slice(P * t, P * (t + 1))
            nc.tensor.matmul_mx(
                out=claim(("C", b, t))[:], lhsT=ab_words[g][:, cols].bitcast(FP8X4), lhsT_scale=ab_scales[g][:, cols],
                rhs=ab_words[GROUPS + c][:].bitcast(FP8X4), rhs_scale=ab_scales[GROUPS + c][:], start=True, stop=True,
            )

        def finish(b, t, engine):
            g, c = BLOCKS[b]
            nc.vector.scalar_tensor_tensor(
                out=scores[b % 3][:, t, :], in0=held[("C", b, t)][:], scalar=gain_cols[:, g, t : t + 1],
                in1=terms[(PACK * b + t) % 16][:], op0=ALU.mult, op1=ALU.add,
            )

        def turn_scores(b, a, engine):
            transposes(("Y", b, a), [scores[b % 3][:, t, P * a : P * (a + 1)] for t in range(PACK)])

        def copy_scores(b, a, engine):
            rows = score_rows[(PACK * b + a) % 12]
            copy(engine, rows[:].rearrange("i (p t) -> i p t", t=PACK), held[("Y", b, a)][:].rearrange("i (t p) -> i p t", t=PACK))

        def store_scores(b, a, engine):
            g, c = BLOCKS[b]
            row0 = SPAN * c + P * a
            nc.sync.dma_start(out=out_0[row0 : row0 + P, SPAN * g : SPAN * (g + 1)], in_=score_rows[(PACK * b + a) % 12][:])

        def group_scores(b, part, engine):
            cols = slice(SPAN // PARTS * part, SPAN // PARTS * (part + 1))
            copy(engine, y_grouped[b % 3][:, cols, :], scores[b % 3][:, :, cols].rearrange("p t i -> p i t"))

        def quantize_scores(b, engine):
            g, c = BLOCKS[b]
            quantize(y_words[b][:], y_scales[g][:, SPAN * c : SPAN * (c + 1)], y_grouped[b % 3][:].rearrange("p i t -> p (i t)"))

        def store_words(b, engine):
            g, c = BLOCKS[b]
            dst = out_1[g].rearrange("p n t -> p (n t)")[:, PACK * SPAN * c : PACK * SPAN * (c + 1)]
            nc.sync.dma_start(out=dst.bitcast(I32), in_=y_words[b][:].bitcast(I32))

        def store_scales(g, q, engine):
            nc.sync.dma_start(
                out=out_2[g, 4 * q : 4 * q + 4, :].bitcast(I32), in_=y_scales[g][32 * q : 32 * q + 4, :].bitcast(I32)
            )

        steps = {
            "w": widen_weight, "W": spread_weight, "W.c": copy_weight,
            "E": turn_enrol, "E.c": copy_enrol, "E.q": quantize_enrol,
            "P": project, "P.s": sum_squares, "P.m": weigh,
            "A": turn_scaled, "A.c": copy_scaled, "A.q": quantize_scaled,
            "X": spread_self_x, "X.c": copy_self_x, "H": make_shift, "T": make_term,
            "C": cross, "C.y": finish, "Y": turn_scores, "Y.c": copy_scores, "Y.d": store_scores,
            "I": group_scores, "Q": quantize_scores, "Q.d": store_words, "Z": store_scales,
        }

        nc.vector.memset(w_scales[:].rearrange("p h n -> p (h n)").bitcast(I32), 0)
        nc.vector.memset(x_scales[:].rearrange("p h n -> p (h n)").bitcast(I32), 0)
        make_identity(nc, ident[:])
        load_enrol(0, 0, 1)
        nc.sync.dma_start(out=weight_raw[0][:], in_=w_enrol.rearrange("(p t) -> p t", t=PACK))
        nc.sync.dma_start(out=w_words[:].bitcast(I32), in_=proj_words.rearrange("h p n -> p h n").bitcast(I32))
        load_enrol(0, 1, 2)
        load_scales(w_scales, proj_scales)
        load_enrol(0, 2, 4)
        nc.sync.dma_start(out=weight_raw[1][:], in_=w_test.rearrange("(p t) -> p t", t=PACK))
        load_scales(x_scales, test_scales)
        load_test(0)
        load_test(1)
        nc.sync.dma_start(out=offset_cols[:], in_=offset.rearrange("(g p t) -> p g t", g=GROUPS, t=PACK))
        nc.sync.dma_start(out=gain_cols[:], in_=gain.rearrange("(g p t) -> p g t", g=GROUPS, t=PACK))
        load_enrol(1, 0, 2)
        load_enrol(1, 2, 4)
        load_test(2)
        load_test(3)

        for token in ORDER.split():
            engine = token[-1] if token[-1] in "SVG" else ""
            body = token[: len(token) - len(engine)]
            name, dot, tail = (body + ".").split(".")[0], "." if "." in body else "", (body + ".").split(".")[1]
            steps[name[0] + dot + tail](*[int(ch) for ch in name[1:]], engine)
